import numpy as np, ml_dtypes
CORES = [40,64,80,88,96,104,120,144]
N = 8
BF = ml_dtypes.bfloat16
def gentries(a):
    return np.ascontiguousarray(a.reshape(8, 16, -1).transpose(0, 2, 1)).reshape(8, -1)
def gtable(e):
    e = np.asarray(e); return np.ascontiguousarray(e.reshape(8, -1, 16).transpose(0, 2, 1)).reshape(128, -1).astype(np.int32)
V, S, G, OFF, DEP, Q = 2048, 1536, 256, (1, 2, 6, 7), 4, 9
B = len(OFF); W = S + B * G
def parts(rng):
    h = rng.integers(0, 128, (N, 8, 16, V)); v = rng.integers(0, 128, (N, 8, 16, S))
    e = rng.integers(0, 16, (N, 8, V)); k0 = rng.integers(0, V, (N, 8, V)); k1 = rng.integers(0, V, (N, 8, V))
    p = rng.integers(0, W, (N, 8, 16, S)); n = rng.integers(0, V, (N, 8, S))
    b = np.ascontiguousarray(np.argsort(rng.random((N, 8, B, S)), axis=-1)[..., :G])
    return h, v, e, k0, k1, p, n, b
def pack(h, v, e, k0, k1, p, n, b):
    return {"hist": np.ascontiguousarray(h.reshape(N, 128, V)).astype(np.float32).astype(BF), "x": np.ascontiguousarray(v.reshape(N, 128, S)).astype(np.float32).astype(BF),
            "way": e.astype(np.int32), "kid0": k0.astype(np.int32), "kid1": k1.astype(np.int32), "nb": np.ascontiguousarray(p.reshape(N, 128, S)).astype(np.int32),
            "nd0": np.stack([gtable(a) for a in n]), "bd": np.stack([gtable(a.reshape(8, -1)) for a in b])}
def setup_inputs(rng):
    return pack(*parts(rng))
def setup_inputs_ties(rng):
    h, v, e, k0, k1, p, n, b = parts(rng)
    hb = rng.choice(np.array([0, 63, 126]), (1, 8, 16, 1)); xb = rng.choice(np.array([0, 64, 127]), (1, 8, 16, 1))
    hb[0, 0] = 126; xb[0, 0] = 127; hb[0, 1] = 0; xb[0, 1] = 0
    k = rng.choice(np.array([0, 0, 0, 0, Q - 1, Q, Q + 1, 16]), (N, 8, 1, V))
    place = np.argsort(rng.random((N, 8, 16, V)), axis=2)
    h = hb + (place < k); v = np.zeros((N, 8, 16, S), np.int64) + xb
    ends = np.array([0, 1, 126, 127])
    h[:, 6:] = rng.choice(ends, (N, 2, 16, V)); v[:, 6:] = rng.choice(ends, (N, 2, 16, S))
    return pack(h, v, e, k0, k1, p, n, b)
def setup_inputs_alike(rng):
    h, v, e, k0, k1, p, n, b = parts(rng)
    p[:, 1] = np.arange(S); p[:, 2] = rng.integers(S, W, (N, 16, S)); p[:, 3] = rng.integers(0, S, (N, 16, S))
    p[:, 4] = rng.choice(np.array([0, S - 1, S, S + G - 1, W - G, W - 1]), (N, 16, S)); p[:, 5] = rng.integers(0, W, (N, 1, 1)); p[:, 6] = p[:, 6, :1]
    b[:, ::2] = rng.choice(np.array([0, S - 1, S // 2, 3]), (N, 4, B, G))
    e[:, 2:4] = rng.integers(0, 16, (N, 2, 1))
    b[:, 0] = rng.integers(1, S, (N, B, 1)); b[:, 7] = np.argsort(rng.random((N, S)), axis=-1)[:, :B * G].reshape(N, B, G)
    n[:, ::7] = np.argsort(rng.random((N, 2, V)), axis=-1)[..., :S]
    return pack(h, v, e, k0, k1, p, n, b)
def setup_inputs_meet(rng):
    h, v, e, k0, k1, p, n, b = parts(rng)
    n[:, :4] = rng.choice(np.array([0, 1, V // 2, V - 1]), (N, 4, S)); n[:, 0] = 0; n[:, 7] = V - 1 - rng.integers(0, 32, (N, S))
    k1[:, 2] = k0[:, 2]; k0[:, 3] = np.arange(V); k1[:, 3] = np.arange(V); k0[:, 4] = np.arange(V)
    k0[:, 5] = rng.choice(np.array([0, V - 1]), (N, V)); k1[:, 5] = rng.choice(np.array([0, V - 1]), (N, V))
    e[:, 6] = rng.choice(np.array([0, 15]), (N, V))
    return pack(h, v, e, k0, k1, p, n, b)
def setup_inputs_far(rng):
    h, v, e, k0, k1, p, n, b = parts(rng); half = V // 2
    h = rng.integers(0, 97, (N, 8, 1, 1)) + rng.integers(0, 31, h.shape); v = rng.integers(0, 97, (N, 8, 1, 1)) + rng.integers(0, 31, v.shape)
    p = rng.integers(S, W, p.shape); b[..., 0] = 0; b[..., G - 1] = S - 1
    e[:, :4] = rng.integers(0, 16, (N, 4, 1)); p[:, :2] = rng.integers(S, S + G, (N, 2, 16, S))
    n[:, 0] = rng.integers(0, V, (N, 1)); v[:, 0] = rng.integers(0, 128, (N, 16, S))
    h[:, 0] = rng.integers(0, 32, (N, 16, V)); h[1::2, 0] += 96
    v[:, 1] = rng.integers(0, 32, (N, 16, S)); h[::2, 1] = rng.integers(64, 80, (N // 2, 16, V)); k0[::2, 1] = np.arange(V)
    h[1::2, 1] = rng.integers(0, 128, (N // 2, 16, V)); h[1::2, 1, :, :half] = rng.integers(0, 16, (N // 2, 16, half))
    n[1::2, 1] = rng.integers(0, half, (N // 2, S))
    k0[1::2, 1, :half] = rng.integers(half, V, (N // 2, half)); k1[1::2, 1, :half] = rng.integers(half, V, (N // 2, half))
    return pack(h, v, e, k0, k1, p, n, b)
def setup_inputs_spread(rng):
    h, v, e, k0, k1, p, n, b = parts(rng)
    h = np.minimum((np.exp2(7 * rng.random((N, 8, 1, V))) * rng.random(h.shape)).astype(np.int64), 127)
    v = np.minimum((np.exp2(7 * rng.random((N, 8, 1, S))) * rng.random(v.shape)).astype(np.int64), 127)
    n = np.minimum((V * rng.random(n.shape) ** 3).astype(np.int64), V - 1); k1 = np.minimum((V * rng.random(k1.shape) ** 2).astype(np.int64), V - 1)
    p = W - 1 - np.minimum((W * rng.random(p.shape) ** 2).astype(np.int64), W - 1)
    b[:, ::2] = np.argsort(rng.random((N, 4, B, S // 2)), axis=-1)[..., :G] + S // 2 * rng.integers(0, 2, (N, 4, B, 1))
    return pack(h, v, e, k0, k1, p, n, b)
def check_inputs(d):
    bad = []
    for k in ("hist", "x"):
        a = np.asarray(d[k]).astype(np.float32)
        if not np.all((a >= 0) & (a <= 127) & (a == np.floor(a))): bad.append("whole numbers from 0 to 127 in " + k)
    for k, hi in (("way", 15), ("kid0", V - 1), ("kid1", V - 1), ("nb", W - 1), ("nd0", V - 1), ("bd", S - 1)):
        if np.min(d[k]) < 0 or np.max(d[k]) > hi: bad.append("range of " + k)
    return bad
def reference(hist, x, way, kid0, kid1, nb, nd0, bd):
    h = hist.astype(np.float32).astype(np.int32).reshape(N, 8, 16, V); xv = x.astype(np.float32).astype(np.int32).reshape(N, 8, 16, S)
    part = nb.astype(np.int64).reshape(N, 8, 16, S)
    n = np.stack([gentries(a) for a in nd0]).astype(np.int64)
    bl = np.stack([gentries(a) for a in bd]).astype(np.int64).reshape(N, 8, B, G)
    for depth in range(DEP):
        hn = np.stack([np.take_along_axis(h[a], n[a][:, None, :], 2) for a in range(N)])
        new = []
        for a in range(N):
            hw, xw = [hn[a]], [xv[a]]
            for i, d in enumerate(OFF):
                q = (a - d) % N; ix = bl[q, :, i][:, None, :]
                hw.append(np.take_along_axis(hn[q], ix, 2)); xw.append(np.take_along_axis(xv[q], ix, 2))
            hw, xw = np.concatenate(hw, axis=2), np.concatenate(xw, axis=2)
            e = np.take_along_axis(way[a].astype(np.int64), n[a], 1)
            p = np.take_along_axis(part[a], e[:, None, :], 1)
            more = xv[a] + np.take_along_axis(hw, p, 2) > np.take_along_axis(xw, p, 2) + hn[a]
            right = np.add.reduce(more.astype(np.int32), axis=1) >= Q
            new.append(np.where(right, np.take_along_axis(kid1[a], n[a], 1), np.take_along_axis(kid0[a], n[a], 1)))
        n = np.stack(new).astype(np.int64)
    return {"y": n.astype(np.float32)}

@@ -1,0 +1,435 @@
+from concourse.bass import DstId, RemoteDMATransfer
+from concourse.mybir import AluOpType as ALU, ActivationFunctionType as ACT
+
+N, V, S, G, DEP, Q = 8, 2048, 1536, 256, 4, 9
+WORLD = 256
+OFF = (1, 2, 6, 7)
+NB = len(OFF)
+W = S + NB * G
+C = S // 16
+MID = W // 2
+
+CFG = {
+    "three": True,
+    "x": ((0, 48), (72, 96), (48, 72)),
+    "vtab": 3,
+    "open": "Px72-96@a As72-96@a A0-48 Pa72-96@a Ea72-96@a A48-72 G",
+    "wait0": "K L0-48 B0-48 Wp0-48 D0-96 L48-96 B48-96 Wp48-96 Y0-70 Pd70-96@c Po0-96 Wk0-96 Ek0-96 Px0-16@a Px80-96@3",
+    "wait": "Pd70-96@c Px0-16@a Px80-96@3 D0-96 B0-48 Wp0-48 B48-96 Wp48-96 Y0-70 Po0-96 Wk0-96 Ek0-96",
+    "wait3": "Pd66-84@c Pd84-96@2 D0-96 B0-48 Wp0-48 B48-96 Wp48-96 Y0-66 Po0-96 Wk0-96",
+    "step": ("Cs70-96@c C0-40 Pc70-96@c C40-70 Sc70-96@c W0-40@0 Ts0-40 N0-40 M0-40 W40-96@1 As0-16@a Ts40-96 A16-40 "
+             "Pa0-16@a N40-96 M40-96 Ea0-16@a As80-96@3 A40-80 Pa80-96@3 Ea80-96@3 G"),
+    "last": "Cs66-84@c Cs84-96@2 C0-48 Pc66-84@c Pc84-96@2 Sc66-84@c Sc84-96@2 C48-66 F0-48 F66-84 F84-96 F48-66",
+}
+
+BF, F32, I32, U16, F16 = "bfloat16", "float32", "int32", "uint16", "float16"
+SCRATCH = {
+    "hs": ("sbuf", [128, V], BF), "xs": ("sbuf", [128, S], BF), "nb32": ("sbuf", [128, S], I32),
+    "nb16": ("sbuf", [128, S], F16), "nd32": ("sbuf", [128, C], I32), "bd32": ("sbuf", [128, 64], I32),
+    "bdo": ("sbuf", [128, 64], U16), "tk": ("sbuf", [128, 384], I32), "wb": ("sbuf", [128, 128], BF),
+    "pc": ("sbuf", [128, 512], BF), "tab": ("sbuf", [128, V], BF), "tmp": ("sbuf", [128, V], BF),
+    "kt": ("sbuf", [128, V], BF), "rep": ("sbuf", [128, V], BF),
+    "zz": ("sbuf", [128, 128], BF), "km": ("sbuf", [128, 128], BF), "ki": ("sbuf", [128, 1], I32),
+    "ei": ("sbuf", [128, 1], I32), "ec": ("sbuf", [128, 1], F32), "nec": ("sbuf", [128, 1], F32),
+    "sg": ("sbuf", [128, 1], F32), "lo": ("sbuf", [128, 1], F32),
+    "fw": ("sbuf", [128, 144], BF), "fh": ("sbuf", [128, 144], F16), "fd": ("sbuf", [128, 144], BF),
+    "f0": ("sbuf", [128, 144], BF), "idp": ("sbuf", [128, 128], BF), "idn": ("sbuf", [128, 128], BF),
+    "bo": ("sbuf", [128, S], F16), "ko": ("sbuf", [128, S], BF), "cmp": ("sbuf", [128, S], BF),
+    "dn": ("sbuf", [128, S], BF),
+    "d0": ("sbuf", [128, 2 * C], F32), "d1": ("sbuf", [128, 2 * C], F32), "sc": ("sbuf", [128, 2 * C], F32),
+    "yt": ("sbuf", [128, C], F32), "yu": ("sbuf", [128, C], F32), "yv": ("sbuf", [128, C], F32),
+}
+for _b in "0123acpk":
+    SCRATCH["q" + _b] = ("psum", [128, 512], F32)
+for _b in "23ac":
+    SCRATCH["g" + _b] = ("sbuf", [128, 512], BF)
+for _t in range(DEP):
+    SCRATCH["dw%d" % _t] = ("sbuf", [128, W], BF)
+    SCRATCH["snd%d" % _t] = ("sbuf", [128, NB * G], BF)
+    SCRATCH["no%d" % _t] = ("sbuf", [128, C], U16)
+    SCRATCH["po%d" % _t] = ("sbuf", [128, C], U16)
+SEMAPHORES = (["cv", "cs", "ct", "cg", "sent", "lnd", "lhs", "lx0", "lx1", "lx2", "lnb0", "lnb1", "lway", "lbd", "lkid", "lkt", "ly"]
+              + ["arr%d" % t for t in range(DEP)] + ["hop%d_%d" % (t, b) for t in range(DEP) for b in range(NB)])
+KEPT = {}
+
+
+def bits(engs):
+    m = 0
+    for e in engs:
+        m |= 1 << e
+    return m
+
+
+def routes(T, topo):
+    if "via" in KEPT:
+        return KEPT["via"]
+    cores = T.cores
+    place = lambda c: (topo.host(c), topo.chip(c))
+    near = [place([c for c in range(WORLD) if topo.mates(cores[q], c)][0]) for q in range(N)]
+    plans = [{}]
+    for q in range(N):
+        src = cores[q]
+        cross = [b for b in range(NB) if not topo.may_write(src, cores[(q + OFF[b]) % N])]
+        able = [c for c in topo.cores_of(src) if all(topo.may_write(c, cores[(q + OFF[b]) % N]) for b in cross)]
+        able.sort(key=lambda c: topo.die(c) != topo.die(src))
+        same = len([c for c in able if topo.die(c) == topo.die(src)])
+        turns = [cross[k:] + cross[:k] for k in range(len(cross))] if len(cross) > same else [cross]
+        grown = []
+        for plan in plans:
+            for turn in turns:
+                p = dict(plan)
+                for b in range(NB):
+                    p[(q, b)] = able[turn.index(b)] if b in turn else None
+                grown.append(p)
+        plans = grown
+
+    def cost(plan):
+        load = {}
+        for (q, b), c in plan.items():
+            src, dst = cores[q], cores[(q + OFF[b]) % N]
+            if c is None:
+                ways = [("out", place(src)), ("in", place(dst))]
+            elif topo.mates(src, dst):
+                ways = [("mate", place(src))]
+            else:
+                ways = [("mate", place(src)), ("out", near[q]), ("in", place(dst))]
+            for w in ways:
+                k = w + (topo.die(src if c is None else c),)
+                load[k] = load.get(k, 0) + (1 if c is None else 2)
+        return (max(load.values()), sum(v * v for v in load.values()))
+
+    KEPT["via"] = min(plans, key=cost)
+    return KEPT["via"]
+
+
+def sends(T, topo, via, q):
+    src = T.cores[q]
+    dest = lambda b: T.cores[(q + OFF[b]) % N]
+    direct = [b for b in range(NB) if via[(q, b)] is None]
+    cross = sorted([b for b in range(NB) if b not in direct],
+                   key=lambda b: (topo.die(via[(q, b)]) == topo.die(src), topo.mates(src, dest(b))))
+    order = cross + direct
+    off = topo.engines(src, dest(direct[0]))
+    on = [e for e in topo.engines(src, via[(q, cross[0])]) if e not in off]
+    if CFG["three"] and len(cross) == 3:
+        groups = [order[:2], order[2:3], order[3:]]
+    else:
+        groups = [order[:2], order[2:]]
+    calls = []
+    for grp in groups:
+        size = (len(on) + len(off)) // len(grp)
+        ndir = len([b for b in grp if b in direct])
+        pool = list(off)
+        call = []
+        for b in grp:
+            if b in direct:
+                k = min(size, len(off) // ndir)
+                call.append((b, dest(b), pool[:k]))
+                pool = pool[k:]
+        rest = list(on) + pool
+        for b in grp:
+            if b not in direct:
+                call.append((b, via[(q, b)], rest[:size]))
+                rest = rest[size:]
+        calls.append(call)
+    return order, calls
+
+
+def width(T, topo, via, q, b):
+    return [len(e) for call in sends(T, topo, via, q)[1] for (bb, d, e) in call if bb == b][0]
+
+
+def relay_program(g, core, T, topo, via, mine):
+    total = 0
+    for t in range(DEP):
+        for (q, b) in mine:
+            dst = T.cores[(q + OFF[b]) % N]
+            rid, pid = topo.addr(dst, core)
+            g.wait_ge(T.sem["hop%d_%d" % (t, b)], width(T, topo, via, q, b))
+            g.remote_dma(T["dw%d" % t][:, S + b * G:S + (b + 1) * G], T["snd%d" % t][:, b * G:(b + 1) * G],
+                         T.sem["arr%d" % t], T.sem.sent, pid, rid, topo.mask(core, dst))
+            total += len(topo.engines(core, dst))
+    g.wait_ge(T.sem.sent, total)
+
+
+def rank_program(g, core, T, topo):
+    via = routes(T, topo)
+    rank = T.rank_of(core)
+    if rank is None:
+        mine = [k for k in sorted(via) if via[k] == core]
+        if mine:
+            relay_program(g, core, T, topo, via, mine)
+        return
+
+    eng = {"g": g, "v": g.vector, "s": g.scalar, "t": g.tensor, "y": g.sync}
+    own = {"g": "cg", "v": "cv", "s": "cs", "t": "ct"}
+    known = {k: {} for k in eng}
+    count, waited, wrote, read = {}, {}, {}, {}
+
+    def need(q, events):
+        top = {}
+        for e in events:
+            if known[q].get(e[0], 0) < e[1] and (e[0] not in top or top[e[0]][1] < e[1]):
+                top[e[0]] = e
+        todo = [e for e in top.values() if not any(o[0] != e[0] and o[2].get(e[0], 0) >= e[1] for o in top.values())]
+        for e in todo:
+            eng[q].wait_ge(T.sem[e[0]], e[1])
+            waited[e[0]] = max(waited.get(e[0], 0), e[1])
+            for k, v in e[2].items():
+                known[q][k] = max(known[q].get(k, 0), v)
+
+    def deps(q, rd, wr):
+        ev = [wrote[k] for k in rd if k in wrote]
+        for k in wr:
+            ev += ([wrote[k]] if k in wrote else []) + read.get(k, [])
+        if q == "t":
+            ev = [e for e in ev if e[0] != "ct"]
+        need(q, ev)
+
+    def done(q, sem, n, rd, wr):
+        count[sem] = count.get(sem, 0) + n
+        clock = dict(known[q])
+        clock[sem] = count[sem]
+        e = (sem, count[sem], clock)
+        for k in rd:
+            read.setdefault(k, []).append(e)
+        for k in wr:
+            wrote[k] = e
+            read[k] = []
+
+    def op(q, fn, rd, wr):
+        deps(q, rd, wr)
+        fn().then_inc(T.sem[own[q]], 1)
+        done(q, own[q], 1, rd, wr)
+
+    def dma(q, sem, pairs, rd, wr):
+        deps(q, rd, wr)
+        for o, i in pairs:
+            eng[q].dma_start(o, i).then_inc(T.sem[sem], 16)
+        done(q, sem, 16 * len(pairs), rd, wr)
+
+    def tok(name, c0, c1):
+        return ["%s.%d" % (name, c) for c in range(c0 // 2, (c1 + 1) // 2)]
+
+    vec, act, pe = g.vector, g.scalar, g.tensor
+    order, calls = sends(T, topo, via, rank)
+    for t in range(DEP):
+        sem = "arr%d" % t
+        count[sem] = 0
+        for bb in range(NB):
+            q = (rank - OFF[bb]) % N
+            hop = via[(q, bb)]
+            count[sem] += width(T, topo, via, q, bb) if hop is None else len(topo.engines(hop, core))
+        wrote[sem] = (sem, count[sem], {sem: count[sem]})
+
+    def wrap(out, col, lhs, src, c0, c1):
+        for i in range(16):
+            last = pe.matmul(T[out][:, col:col + c1 - c0], T[lhs][:, 15 - i:143 - i], T[src][:, 16 * c0 + i:16 * c1:16],
+                             i == 0, i == 15)
+        return last
+
+    def flat(out, col, lhs, src, i0, i1, start, stop):
+        for i in range(i0, i1):
+            last = pe.matmul(T[out][:, col:col + C], T[lhs][:, 15 - i:143 - i], T[src][:, C * i:C * (i + 1)],
+                             start and i == i0, stop and i == i1 - 1)
+        return last
+
+    dma("y", "lnd", [(T.nd32[:], T.nd0[:])], [], ["nd32"])
+    dma("s", "lway", [(T.tk[:, 0:128], T.way[:])], [], ["way"])
+    dma("y", "lhs", [(T.hs[:], T.hist[:])], [], ["hs"])
+    dma("s", "lbd", [(T.bd32[:], T.bd[:])], [], ["bd32"])
+    for k, (c0, c1) in enumerate(CFG["x"]):
+        dma("y", "lx%d" % k, [(T.xs[:, 16 * c0:16 * c1], T.x[:, 16 * c0:16 * c1])], [], tok("xs", c0, c1))
+    dma("y", "lkid", [(T.tk[:, 128:256], T.kid0[:]), (T.tk[:, 256:384], T.kid1[:])], [], ["kid"])
+    for k in range(2):
+        dma("y", "lnb%d" % k, [(T.nb32[:, k * S // 2:(k + 1) * S // 2], T.nb[:, k * S // 2:(k + 1) * S // 2])], [],
+            tok("nb32", k * C // 2, (k + 1) * C // 2))
+
+    op("g", lambda: g.iota(T.zz[:], [[-16, 8], [0, 16]], 0, 1, allow_small_or_imprecise_dtypes=True), [], ["zz"])
+    op("g", lambda: g.iota(T.ki[:], [[0, 1]], 0, 1), [], ["ki"])
+    op("g", lambda: g.iota(T.km[:], [[-1, 128]], 0, 1, allow_small_or_imprecise_dtypes=True), [], ["km"])
+    op("v", lambda: vec.memset(T.fw[:], 0.0), [], ["fw"])
+    op("v", lambda: vec.memset(T.d0[:], 0.0), [], ["d0z"])
+    for j in range(16):
+        op("v", lambda: vec.tensor_scalar(T.rep[:, 128 * j:128 * (j + 1)], T.zz[:], float(j), None, ALU.is_equal),
+           ["zz"], ["rep%d" % j])
+        if j == 7:
+            op("v", lambda: vec.tensor_scalar(T.ei[:], T.ki[:], 15, None, ALU.bitwise_and), ["ki"], ["ei"])
+    op("v", lambda: vec.tensor_scalar(T.nec[:], T.ei[:], -1.0, None, ALU.mult), ["ei"], ["nec"])
+    op("v", lambda: vec.tensor_copy(T.wb[:], T.tk[:, 0:128]), ["way"], ["wb"])
+    tb = ["q0", "q1", "q2", "q3"]
+    for k in range(4):
+        def rep4():
+            for j in range(4 * k, 4 * k + 4):
+                last = pe.matmul(T[tb[k]][:, 128 * (j % 4):128 * (j % 4 + 1)], T.rep[:, 128 * j:128 * (j + 1)], T.wb[:],
+                                 True, True)
+            return last
+        op("t", rep4, ["wb"] + ["rep%d" % j for j in range(4 * k, 4 * k + 4)], [tb[k]])
+    for k in range(4):
+        op("s", lambda: act.activation(T.tmp[:, 512 * k:512 * (k + 1)], T[tb[k]][:], ACT.Abs, bias=T.nec[:]),
+           ["nec"], [tb[k], "tmp%d" % k])
+    op("v", lambda: vec.tensor_copy(T.ec[:], T.ei[:]), ["ei"], ["ec"])
+    op("v", lambda: vec.tensor_scalar(T.idp[:], T.km[:], 0.0, None, ALU.is_equal), ["km"], ["idp"])
+    op("v", lambda: vec.tensor_scalar(T.idn[:], T.km[:], 0.0, -1.0, ALU.is_equal, ALU.mult), ["km"], ["idn"])
+    op("v", lambda: vec.tensor_copy(T.no0[:], T.nd32[:]), ["nd32"], tok("no0", 0, C))
+    op("v", lambda: vec.tensor_scalar(T.fw[:, 15:143:16], T.zz[:, 0:128:16], T.ec[:], None, ALU.is_equal),
+       ["zz", "ec"], ["fw"])
+    op("v", lambda: vec.tensor_scalar(T.sg[:], T.ec[:], 1.5, 0.5, ALU.is_ge, ALU.subtract), ["ec"], ["sg"])
+    op("v", lambda: vec.tensor_scalar(T.lo[:], T.ec[:], 1.5, None, ALU.is_lt), ["ec"], ["lo"])
+    for k, bb in enumerate(order):
+        op("v", lambda: vec.tensor_copy(T.bdo[:, 16 * k:16 * (k + 1)], T.bd32[:, 16 * bb:16 * (bb + 1)]), ["bd32"], ["bdo%d" % k])
+    op("v", lambda: vec.tensor_copy(T.fh[:], T.fw[:]), ["fw"], ["fh"])
+    op("v", lambda: vec.tensor_scalar(T.fd[:], T.fw[:], T.sg[:], 2.0, ALU.mult, ALU.mult), ["fw", "sg"], ["fd"])
+    op("v", lambda: vec.tensor_scalar(T.f0[:], T.fw[:], T.lo[:], None, ALU.mult), ["fw", "lo"], ["f0"])
+    op("v", lambda: vec.memset(T.kt[:], 0.0), [], ["kt"])
+    cut = 512 * CFG["vtab"]
+    op("v", lambda: vec.tensor_scalar(T.tab[:, 0:cut], T.tmp[:, 0:cut], 0.0, None, ALU.is_equal),
+       ["tmp%d" % k for k in range(CFG["vtab"])], ["tabv"])
+
+    held, begun = {}, []
+
+    def border(r):
+        for pos in range(NB):
+            cuts = [(0, 8, "v"), (8, 16, "s")] if len(calls) == 3 and pos >= 2 else [(0, 16, "vs"[pos % 2])]
+            for a, b, who in cuts:
+                out = T["snd" + r][:, pos * G + 16 * a:pos * G + 16 * b]
+                src = T["dw" + r][:, 0:S].indirect(T.bdo[:, 16 * pos + a:16 * pos + b])
+                rd, wr = tok("dw" + r, 0, C) + ["bdo%d" % pos], tok("snd" + r, 16 * pos + a, 16 * pos + b)
+                if who == "v":
+                    op("v", lambda: vec.tensor_copy(out, src), rd, wr)
+                else:
+                    op("s", lambda: act.activation(out, src, ACT.Copy), rd, wr)
+        for call in calls:
+            trs, rd = [], []
+            for (bb, d, e) in call:
+                rid, pid = topo.addr(d, core)
+                pos = order.index(bb)
+                rd += tok("snd" + r, 16 * pos, 16 * pos + 16)
+                if via[(rank, bb)] is None:
+                    dst, sem = T["dw" + r][:, S + bb * G:S + (bb + 1) * G], "arr" + r
+                else:
+                    dst, sem = T["snd" + r][:, bb * G:(bb + 1) * G], "hop%s_%d" % (r, bb)
+                trs.append(RemoteDMATransfer(dst_ids=[DstId(rid=rid, pnc=pid)], dma_engine_mask=bits(e), remote_sem=T.sem[sem],
+                                             src=T["snd" + r][:, pos * G:(pos + 1) * G], dst=dst))
+                count["sent"] = count.get("sent", 0) + len(e)
+            deps("g", rd, [])
+            g.remote_dma_fused(trs, local_sem=T.sem.sent)
+
+    def stem(word):
+        return word.split("@")[0].rstrip("0123456789-")
+
+    def emit(word, t):
+        name = stem(word)
+        r = str(t)
+        if name == "G":
+            border(r)
+            return
+        if name == "K":
+            op("v", lambda: vec.tensor_copy(T.pc[:, 0:256], T.tk[:, 128:384]), ["kid"], ["pch"])
+            op("v", lambda: vec.tensor_tensor(T.pc[:, 256:512], T.tk[:, 128:384], T.pc[:, 0:256], ALU.subtract),
+               ["kid", "pch"], ["pcl"])
+            dma("y", "lkt", [(T.kt[i:128:16, :], T.pc[:, 128 * k:128 * (k + 1)]) for i, k in enumerate((0, 2, 1, 3))],
+                ["pch", "pcl"], ["kt"])
+            return
+        span = word[len(name):].split("@")
+        c0, c1 = [int(v) for v in span[0].split("-")]
+        last = t == DEP - 1
+        n = 16 * (c1 - c0)
+        e0, e1 = 16 * c0, 16 * c1
+        no, po, dw = T["no" + r], T["po" + r], T["dw" + r]
+        window = ["arr" + r] + tok("dw" + r, 0, C)
+        qn, gn = "q" + span[-1], "g" + span[-1]
+        if name == "L":
+            op("v", lambda: vec.tensor_scalar(T.nb16[:, e0:e1], T.nb32[:, e0:e1], float(MID), None, ALU.subtract),
+               tok("nb32", c0, c1), tok("nb16", c0, c1))
+        if name == "A":
+            op("v", lambda: vec.tensor_tensor(dw[:, e0:e1], T.hs[:].indirect(no[:, c0:c1]), T.xs[:, e0:e1], ALU.subtract),
+               ["hs"] + tok("xs", c0, c1) + tok("no" + r, c0, c1), tok("dw" + r, c0, c1))
+        if name == "Px":
+            op("t", lambda: pe.matmul(T[qn][:, 0:n], T.idn[:], T.xs[:, e0:e1], True, False), ["idn"] + tok("xs", c0, c1), [qn])
+        if name == "As":
+            op("s", lambda: act.activation(T[gn][:, 0:n], T.hs[:].indirect(no[:, c0:c1]), ACT.Copy),
+               ["hs"] + tok("no" + r, c0, c1), [gn])
+        if name in ("Pa", "Pc"):
+            op("t", lambda: pe.matmul(T[qn][:, 0:n], T.idp[:], T[gn][:, 0:n], False, True), ["idp", gn], [qn])
+        if name == "Ea":
+            op("s", lambda: act.activation(dw[:, e0:e1], T[qn][:, 0:n], ACT.Copy), [], [qn] + tok("dw" + r, c0, c1))
+        if name == "Y":
+            op("v", lambda: vec.tensor_copy(T.dn[:, e0:e1], dw[:, e0:e1]), tok("dw" + r, c0, c1), tok("dn", c0, c1))
+        if name == "B":
+            op("v", lambda: vec.tensor_tensor(T.bo[:, e0:e1], T.tab[:].indirect(no[:, c0:c1]), T.nb16[:, e0:e1], ALU.mult),
+               ["tabv", "tabs"] + tok("nb16", c0, c1) + tok("no" + r, c0, c1), tok("bo", c0, c1))
+        if name == "Wp":
+            op("t", lambda: wrap("qp", c0, "fh", "bo", c0, c1), ["fh"] + tok("bo", c0, c1), ["qp"])
+        if name == "Po":
+            op("v", lambda: vec.tensor_scalar(po[:, c0:c1], T.qp[:, c0:c1], float(MID), None, ALU.add), [],
+               ["qp"] + tok("po" + r, c0, c1))
+        if name == "D":
+            op("s", lambda: act.activation(T.ko[:, e0:e1], T.kt[:].indirect(no[:, c0:c1]), ACT.Copy),
+               ["kt"] + tok("no" + r, c0, c1), tok("ko", c0, c1))
+        if name == "Wk":
+            for col, lhs in ((c0, "fd"), (C + c0, "f0")):
+                if last:
+                    op("t", lambda: flat("qk", col - c0, lhs, "ko", 0, 16, True, True), [lhs] + tok("ko", 0, C), ["qk"])
+                else:
+                    op("t", lambda: wrap("qk", col, lhs, "ko", c0, c1), [lhs] + tok("ko", c0, c1), ["qk"])
+        if name == "Ek":
+            op("s", lambda: act.activation(T.d0[:, 2 * c0 + 1:2 * c1:2], T.qk[:, c0:c1], ACT.Copy), ["d0z"],
+               ["qk"] + tok("d0", c0, c1))
+            op("s", lambda: act.activation(T.d1[:, 2 * c0 + 1:2 * c1:2], T.qk[:, C + c0:C + c1], ACT.Copy), [],
+               ["qk"] + tok("d1m", c0, c1))
+        if name == "C":
+            op("v", lambda: vec.tensor_tensor(T.cmp[:, e0:e1], dw[:].indirect(po[:, c0:c1]), T.dn[:, e0:e1], ALU.is_gt),
+               window + tok("dn", c0, c1) + tok("po" + r, c0, c1), tok("cmp", c0, c1))
+        if name == "Pd":
+            op("t", lambda: pe.matmul(T[qn][:, 0:n], T.idn[:], dw[:, e0:e1], True, False), ["idn"] + tok("dw" + r, c0, c1), [qn])
+        if name == "Cs":
+            op("s", lambda: act.activation(T[gn][:, 0:n], dw[:].indirect(po[:, c0:c1]), ACT.Copy),
+               window + tok("po" + r, c0, c1), [gn])
+        if name == "Sc":
+            op("s", lambda: act.activation(T.cmp[:, e0:e1], T[qn][:, 0:n], ACT.Sigmoid, bias=-100.0, scale=200.0), [],
+               [qn] + tok("cmp", c0, c1))
+        if name == "W":
+            for c in range(c0, c1):
+                held[c] = (qn, c0)
+            op("t", lambda: wrap(qn, 0, "fw", "cmp", c0, c1), ["fw"] + tok("cmp", c0, c1), [qn])
+        if name in ("Tv", "Ts"):
+            bank, base = held[c0]
+            out, src = T.d1[:, 2 * c0:2 * c1:2], T[bank][:, c0 - base:c1 - base]
+            if name == "Tv":
+                op("v", lambda: vec.tensor_scalar(out, src, Q - 0.5, None, ALU.is_ge), [], [bank] + tok("d1s", c0, c1))
+            else:
+                op("s", lambda: act.activation(out, src, ACT.Sigmoid, bias=-200.0 * (Q - 0.5), scale=200.0), [],
+                   [bank] + tok("d1s", c0, c1))
+        if name == "N":
+            op("v", lambda: vec.tensor_tensor_scan(T.sc[:, 2 * c0:2 * c1], T.d0[:, 2 * c0:2 * c1], T.d1[:, 2 * c0:2 * c1],
+                                                   0.0, ALU.mult, ALU.add),
+               tok("d0", c0, c1) + tok("d1m", c0, c1) + tok("d1s", c0, c1), tok("sc", c0, c1))
+        if name == "M":
+            op("v", lambda: vec.tensor_scalar(no[:, c0:c1], T.sc[:, 2 * c0 + 1:2 * c1:2], 0.25, None, ALU.add),
+               tok("sc", c0, c1), tok("no" + r, c0, c1))
+        if name == "F":
+            begun.append(c1 - c0)
+            op("t", lambda: flat("q0", 0, "fw", "cmp", c0 // 6, c1 // 6, len(begun) == 1, sum(begun) == C),
+               ["fw"] + tok("cmp", c0, c1), ["q0"])
+
+    for w in CFG["open"].split():
+        emit(w, 0)
+    op("s", lambda: act.activation(T.tab[:, cut:V], T.tmp[:, cut:V], ACT.Sigmoid, bias=100.0, scale=-200.0),
+       ["tmp%d" % k for k in range(4)], ["tabs"])
+    for w in CFG["wait0"].split():
+        emit(w, 0)
+    for t in range(DEP - 1):
+        for w in CFG["step"].split():
+            emit(w, t if stem(w) in ("C", "Cs", "Pc", "Sc", "W", "Tv", "Ts", "N") else t + 1)
+        for w in CFG["wait3" if t == DEP - 2 else "wait"].split():
+            emit(w, t + 1)
+    for w in CFG["last"].split():
+        emit(w, DEP - 1)
+    op("v", lambda: vec.tensor_scalar(T.yt[:], T.q0[:, 0:C], Q - 0.5, None, ALU.is_ge), [], ["q0", "yt"])
+    op("v", lambda: vec.tensor_tensor(T.yu[:], T.yt[:], T.qk[:, 0:C], ALU.mult), ["yt"], ["qk", "yu"])
+    op("v", lambda: vec.tensor_tensor(T.yv[:], T.yu[:], T.qk[:, C:2 * C], ALU.add), ["yu"], ["qk", "yv"])
+    dma("y", "ly", [(T.y[:], T.yv[:])], ["yv"], ["y"])
+    for sem in sorted(count, key=lambda s: s == "ly"):
+        if waited.get(sem, 0) < count[sem]:
+            g.wait_ge(T.sem[sem], count[sem])

@@ -12,13 +12,12 @@ MID = W // 2
 CFG = {
     "three": True,
     "x": ((0, 48), (72, 96), (48, 72)),
-    "vtab": 3,
-    "open": "Px72-96@a As72-96@a A0-48 Pa72-96@a Ea72-96@a A48-72 G",
-    "wait0": "K L0-48 B0-48 Wp0-48 D0-96 L48-96 B48-96 Wp48-96 Y0-70 Pd70-96@c Po0-96 Wk0-96 Ek0-96 Px0-16@a Px80-96@3",
-    "wait": "Pd70-96@c Px0-16@a Px80-96@3 D0-96 B0-48 Wp0-48 B48-96 Wp48-96 Y0-70 Po0-96 Wk0-96 Ek0-96",
+    "open": "Px72-96@a As72-96@a Z3 A0-48 Pa72-96@a Ea72-96@a A48-72 G",
+    "wait0": "K L0-48 B0-48 Wp0-48 D0-96 L48-96 B48-96 Wp48-96 Y0-72 Px0-16@a Px82-96@3 Pd72-96@c Po0-96 Wk0-96",
+    "wait": "Pd72-96@c Px0-16@a Px82-96@3 D0-96 B0-48 Wp0-48 B48-96 Wp48-96 Y0-72 Po0-96 Wk0-96",
     "wait3": "Pd66-84@c Pd84-96@2 D0-96 B0-48 Wp0-48 B48-96 Wp48-96 Y0-66 Po0-96 Wk0-96",
-    "step": ("Cs70-96@c C0-40 Pc70-96@c C40-70 Sc70-96@c W0-40@0 Ts0-40 N0-40 M0-40 W40-96@1 As0-16@a Ts40-96 A16-40 "
-             "Pa0-16@a N40-96 M40-96 Ea0-16@a As80-96@3 A40-80 Pa80-96@3 Ea80-96@3 G"),
+    "step": ("Cs72-96@c Ek0-96 C0-40 Pc72-96@c C40-72 Sc72-96@c W0-40@0 Ts0-40 N0-40 M0-40 W40-96@1 As0-16@a Ts40-96 A16-40 "
+             "Pa0-16@a N40-96 M40-96 Ea0-16@a As82-96@3 A40-82 Pa82-96@3 Ea82-96@3 G"),
     "last": "Cs66-84@c Cs84-96@2 C0-48 Pc66-84@c Pc84-96@2 Sc66-84@c Sc84-96@2 C48-66 F0-48 F66-84 F84-96 F48-66",
 }
 
@@ -248,6 +247,7 @@ def rank_program(g, core, T, topo):
     op("g", lambda: g.iota(T.zz[:], [[-16, 8], [0, 16]], 0, 1, allow_small_or_imprecise_dtypes=True), [], ["zz"])
     op("g", lambda: g.iota(T.ki[:], [[0, 1]], 0, 1), [], ["ki"])
     op("g", lambda: g.iota(T.km[:], [[-1, 128]], 0, 1, allow_small_or_imprecise_dtypes=True), [], ["km"])
+    op("g", lambda: g.iota(T.kt[:], [[0, V]], 0, 0, allow_small_or_imprecise_dtypes=True), [], ["kt"])
     op("v", lambda: vec.memset(T.fw[:], 0.0), [], ["fw"])
     op("v", lambda: vec.memset(T.d0[:], 0.0), [], ["d0z"])
     for j in range(16):
@@ -265,9 +265,13 @@ def rank_program(g, core, T, topo):
                                  True, True)
             return last
         op("t", rep4, ["wb"] + ["rep%d" % j for j in range(4 * k, 4 * k + 4)], [tb[k]])
-    for k in range(4):
+
+    def apart(k):
         op("s", lambda: act.activation(T.tmp[:, 512 * k:512 * (k + 1)], T[tb[k]][:], ACT.Abs, bias=T.nec[:]),
            ["nec"], [tb[k], "tmp%d" % k])
+
+    for k in range(3):
+        apart(k)
     op("v", lambda: vec.tensor_copy(T.ec[:], T.ei[:]), ["ei"], ["ec"])
     op("v", lambda: vec.tensor_scalar(T.idp[:], T.km[:], 0.0, None, ALU.is_equal), ["km"], ["idp"])
     op("v", lambda: vec.tensor_scalar(T.idn[:], T.km[:], 0.0, -1.0, ALU.is_equal, ALU.mult), ["km"], ["idn"])
@@ -281,10 +285,7 @@ def rank_program(g, core, T, topo):
     op("v", lambda: vec.tensor_copy(T.fh[:], T.fw[:]), ["fw"], ["fh"])
     op("v", lambda: vec.tensor_scalar(T.fd[:], T.fw[:], T.sg[:], 2.0, ALU.mult, ALU.mult), ["fw", "sg"], ["fd"])
     op("v", lambda: vec.tensor_scalar(T.f0[:], T.fw[:], T.lo[:], None, ALU.mult), ["fw", "lo"], ["f0"])
-    op("v", lambda: vec.memset(T.kt[:], 0.0), [], ["kt"])
-    cut = 512 * CFG["vtab"]
-    op("v", lambda: vec.tensor_scalar(T.tab[:, 0:cut], T.tmp[:, 0:cut], 0.0, None, ALU.is_equal),
-       ["tmp%d" % k for k in range(CFG["vtab"])], ["tabv"])
+    op("v", lambda: vec.tensor_scalar(T.tab[:, 0:1024], T.tmp[:, 0:1024], 0.0, None, ALU.is_equal), ["tmp0", "tmp1"], ["tabv"])
 
     held, begun = {}, []
 
@@ -321,11 +322,15 @@ def rank_program(g, core, T, topo):
     def emit(word, t):
         name = stem(word)
         r = str(t)
+        if name == "Z":
+            apart(int(word[1:]))
+            return
         if name == "G":
             border(r)
             return
         if name == "K":
             op("v", lambda: vec.tensor_copy(T.pc[:, 0:256], T.tk[:, 128:384]), ["kid"], ["pch"])
+            op("v", lambda: vec.tensor_scalar(T.tab[:, 1024:1536], T.tmp[:, 1024:1536], 0.0, None, ALU.is_equal), ["tmp2"], ["tabw"])
             op("v", lambda: vec.tensor_tensor(T.pc[:, 256:512], T.tk[:, 128:384], T.pc[:, 0:256], ALU.subtract),
                ["kid", "pch"], ["pcl"])
             dma("y", "lkt", [(T.kt[i:128:16, :], T.pc[:, 128 * k:128 * (k + 1)]) for i, k in enumerate((0, 2, 1, 3))],
@@ -358,7 +363,7 @@ def rank_program(g, core, T, topo):
             op("v", lambda: vec.tensor_copy(T.dn[:, e0:e1], dw[:, e0:e1]), tok("dw" + r, c0, c1), tok("dn", c0, c1))
         if name == "B":
             op("v", lambda: vec.tensor_tensor(T.bo[:, e0:e1], T.tab[:].indirect(no[:, c0:c1]), T.nb16[:, e0:e1], ALU.mult),
-               ["tabv", "tabs"] + tok("nb16", c0, c1) + tok("no" + r, c0, c1), tok("bo", c0, c1))
+               ["tabv", "tabw", "tabs"] + tok("nb16", c0, c1) + tok("no" + r, c0, c1), tok("bo", c0, c1))
         if name == "Wp":
             op("t", lambda: wrap("qp", c0, "fh", "bo", c0, c1), ["fh"] + tok("bo", c0, c1), ["qp"])
         if name == "Po":
@@ -415,13 +420,12 @@ def rank_program(g, core, T, topo):
 
     for w in CFG["open"].split():
         emit(w, 0)
-    op("s", lambda: act.activation(T.tab[:, cut:V], T.tmp[:, cut:V], ACT.Sigmoid, bias=100.0, scale=-200.0),
-       ["tmp%d" % k for k in range(4)], ["tabs"])
+    op("s", lambda: act.activation(T.tab[:, 1536:V], T.tmp[:, 1536:V], ACT.Sigmoid, bias=100.0, scale=-200.0), ["tmp3"], ["tabs"])
     for w in CFG["wait0"].split():
         emit(w, 0)
     for t in range(DEP - 1):
         for w in CFG["step"].split():
-            emit(w, t if stem(w) in ("C", "Cs", "Pc", "Sc", "W", "Tv", "Ts", "N") else t + 1)
+            emit(w, t if stem(w) in ("C", "Cs", "Ek", "Pc", "Sc", "W", "Tv", "Ts", "N") else t + 1)
         for w in CFG["wait3" if t == DEP - 2 else "wait"].split():
             emit(w, t + 1)
     for w in CFG["last"].split():

from concourse.bass import DstId, RemoteDMATransfer
from concourse.mybir import AluOpType as ALU, ActivationFunctionType as ACT

N, V, S, G, DEP, Q = 8, 2048, 1536, 256, 4, 9
WORLD = 256
OFF = (1, 2, 6, 7)
NB = len(OFF)
W = S + NB * G
C = S // 16
MID = W // 2

CFG = {
    "three": True,
    "x": ((0, 48), (72, 96), (48, 72)),
    "open": "Px72-96@a As72-96@a Z3 A0-48 Pa72-96@a Ea72-96@a A48-72 G",
    "wait0": "K L0-48 B0-48 Wp0-48 D0-96 L48-96 B48-96 Wp48-96 Y0-72 Px0-16@a Px82-96@3 Pd72-96@c Po0-96 Wk0-96",
    "wait": "Pd72-96@c Px0-16@a Px82-96@3 D0-96 B0-48 Wp0-48 B48-96 Wp48-96 Y0-72 Po0-96 Wk0-96",
    "wait3": "Pd66-84@c Pd84-96@2 D0-96 B0-48 Wp0-48 B48-96 Wp48-96 Y0-66 Po0-96 Wk0-96",
    "step": ("Cs72-96@c Ek0-96 C0-40 Pc72-96@c C40-72 Sc72-96@c W0-40@0 Ts0-40 N0-40 M0-40 W40-96@1 As0-16@a Ts40-96 A16-40 "
             "Pa0-16@a N40-96 M40-96 Ea0-16@a As82-96@3 A40-82 Pa82-96@3 Ea82-96@3 G"),
    "last": "Cs66-84@c Cs84-96@2 C0-48 Pc66-84@c Pc84-96@2 Sc66-84@c Sc84-96@2 C48-66 F0-48 F66-84 F84-96 F48-66",
}

BF, F32, I32, U16, F16 = "bfloat16", "float32", "int32", "uint16", "float16"
SCRATCH = {
    "hs": ("sbuf", [128, V], BF), "xs": ("sbuf", [128, S], BF), "nb32": ("sbuf", [128, S], I32),
    "nb16": ("sbuf", [128, S], F16), "nd32": ("sbuf", [128, C], I32), "bd32": ("sbuf", [128, 64], I32),
    "bdo": ("sbuf", [128, 64], U16), "tk": ("sbuf", [128, 384], I32), "wb": ("sbuf", [128, 128], BF),
    "pc": ("sbuf", [128, 512], BF), "tab": ("sbuf", [128, V], BF), "tmp": ("sbuf", [128, V], BF),
    "kt": ("sbuf", [128, V], BF), "rep": ("sbuf", [128, V], BF),
    "zz": ("sbuf", [128, 128], BF), "km": ("sbuf", [128, 128], BF), "ki": ("sbuf", [128, 1], I32),
    "ei": ("sbuf", [128, 1], I32), "ec": ("sbuf", [128, 1], F32), "nec": ("sbuf", [128, 1], F32),
    "sg": ("sbuf", [128, 1], F32), "lo": ("sbuf", [128, 1], F32),
    "fw": ("sbuf", [128, 144], BF), "fh": ("sbuf", [128, 144], F16), "fd": ("sbuf", [128, 144], BF),
    "f0": ("sbuf", [128, 144], BF), "idp": ("sbuf", [128, 128], BF), "idn": ("sbuf", [128, 128], BF),
    "bo": ("sbuf", [128, S], F16), "ko": ("sbuf", [128, S], BF), "cmp": ("sbuf", [128, S], BF),
    "dn": ("sbuf", [128, S], BF),
    "d0": ("sbuf", [128, 2 * C], F32), "d1": ("sbuf", [128, 2 * C], F32), "sc": ("sbuf", [128, 2 * C], F32),
    "yt": ("sbuf", [128, C], F32), "yu": ("sbuf", [128, C], F32), "yv": ("sbuf", [128, C], F32),
}
for _b in "0123acpk":
    SCRATCH["q" + _b] = ("psum", [128, 512], F32)
for _b in "23ac":
    SCRATCH["g" + _b] = ("sbuf", [128, 512], BF)
for _t in range(DEP):
    SCRATCH["dw%d" % _t] = ("sbuf", [128, W], BF)
    SCRATCH["snd%d" % _t] = ("sbuf", [128, NB * G], BF)
    SCRATCH["no%d" % _t] = ("sbuf", [128, C], U16)
    SCRATCH["po%d" % _t] = ("sbuf", [128, C], U16)
SEMAPHORES = (["cv", "cs", "ct", "cg", "sent", "lnd", "lhs", "lx0", "lx1", "lx2", "lnb0", "lnb1", "lway", "lbd", "lkid", "lkt", "ly"]
              + ["arr%d" % t for t in range(DEP)] + ["hop%d_%d" % (t, b) for t in range(DEP) for b in range(NB)])
KEPT = {}


def bits(engs):
    m = 0
    for e in engs:
        m |= 1 << e
    return m


def routes(T, topo):
    if "via" in KEPT:
        return KEPT["via"]
    cores = T.cores
    place = lambda c: (topo.host(c), topo.chip(c))
    near = [place([c for c in range(WORLD) if topo.mates(cores[q], c)][0]) for q in range(N)]
    plans = [{}]
    for q in range(N):
        src = cores[q]
        cross = [b for b in range(NB) if not topo.may_write(src, cores[(q + OFF[b]) % N])]
        able = [c for c in topo.cores_of(src) if all(topo.may_write(c, cores[(q + OFF[b]) % N]) for b in cross)]
        able.sort(key=lambda c: topo.die(c) != topo.die(src))
        same = len([c for c in able if topo.die(c) == topo.die(src)])
        turns = [cross[k:] + cross[:k] for k in range(len(cross))] if len(cross) > same else [cross]
        grown = []
        for plan in plans:
            for turn in turns:
                p = dict(plan)
                for b in range(NB):
                    p[(q, b)] = able[turn.index(b)] if b in turn else None
                grown.append(p)
        plans = grown

    def cost(plan):
        load = {}
        for (q, b), c in plan.items():
            src, dst = cores[q], cores[(q + OFF[b]) % N]
            if c is None:
                ways = [("out", place(src)), ("in", place(dst))]
            elif topo.mates(src, dst):
                ways = [("mate", place(src))]
            else:
                ways = [("mate", place(src)), ("out", near[q]), ("in", place(dst))]
            for w in ways:
                k = w + (topo.die(src if c is None else c),)
                load[k] = load.get(k, 0) + (1 if c is None else 2)
        return (max(load.values()), sum(v * v for v in load.values()))

    KEPT["via"] = min(plans, key=cost)
    return KEPT["via"]


def sends(T, topo, via, q):
    src = T.cores[q]
    dest = lambda b: T.cores[(q + OFF[b]) % N]
    direct = [b for b in range(NB) if via[(q, b)] is None]
    cross = sorted([b for b in range(NB) if b not in direct],
                   key=lambda b: (topo.die(via[(q, b)]) == topo.die(src), topo.mates(src, dest(b))))
    order = cross + direct
    off = topo.engines(src, dest(direct[0]))
    on = [e for e in topo.engines(src, via[(q, cross[0])]) if e not in off]
    if CFG["three"] and len(cross) == 3:
        groups = [order[:2], order[2:3], order[3:]]
    else:
        groups = [order[:2], order[2:]]
    calls = []
    for grp in groups:
        size = (len(on) + len(off)) // len(grp)
        ndir = len([b for b in grp if b in direct])
        pool = list(off)
        call = []
        for b in grp:
            if b in direct:
                k = min(size, len(off) // ndir)
                call.append((b, dest(b), pool[:k]))
                pool = pool[k:]
        rest = list(on) + pool
        for b in grp:
            if b not in direct:
                call.append((b, via[(q, b)], rest[:size]))
                rest = rest[size:]
        calls.append(call)
    return order, calls


def width(T, topo, via, q, b):
    return [len(e) for call in sends(T, topo, via, q)[1] for (bb, d, e) in call if bb == b][0]


def relay_program(g, core, T, topo, via, mine):
    total = 0
    for t in range(DEP):
        for (q, b) in mine:
            dst = T.cores[(q + OFF[b]) % N]
            rid, pid = topo.addr(dst, core)
            g.wait_ge(T.sem["hop%d_%d" % (t, b)], width(T, topo, via, q, b))
            g.remote_dma(T["dw%d" % t][:, S + b * G:S + (b + 1) * G], T["snd%d" % t][:, b * G:(b + 1) * G],
                         T.sem["arr%d" % t], T.sem.sent, pid, rid, topo.mask(core, dst))
            total += len(topo.engines(core, dst))
    g.wait_ge(T.sem.sent, total)


def rank_program(g, core, T, topo):
    via = routes(T, topo)
    rank = T.rank_of(core)
    if rank is None:
        mine = [k for k in sorted(via) if via[k] == core]
        if mine:
            relay_program(g, core, T, topo, via, mine)
        return

    eng = {"g": g, "v": g.vector, "s": g.scalar, "t": g.tensor, "y": g.sync}
    own = {"g": "cg", "v": "cv", "s": "cs", "t": "ct"}
    known = {k: {} for k in eng}
    count, waited, wrote, read = {}, {}, {}, {}

    def need(q, events):
        top = {}
        for e in events:
            if known[q].get(e[0], 0) < e[1] and (e[0] not in top or top[e[0]][1] < e[1]):
                top[e[0]] = e
        todo = [e for e in top.values() if not any(o[0] != e[0] and o[2].get(e[0], 0) >= e[1] for o in top.values())]
        for e in todo:
            eng[q].wait_ge(T.sem[e[0]], e[1])
            waited[e[0]] = max(waited.get(e[0], 0), e[1])
            for k, v in e[2].items():
                known[q][k] = max(known[q].get(k, 0), v)

    def deps(q, rd, wr):
        ev = [wrote[k] for k in rd if k in wrote]
        for k in wr:
            ev += ([wrote[k]] if k in wrote else []) + read.get(k, [])
        if q == "t":
            ev = [e for e in ev if e[0] != "ct"]
        need(q, ev)

    def done(q, sem, n, rd, wr):
        count[sem] = count.get(sem, 0) + n
        clock = dict(known[q])
        clock[sem] = count[sem]
        e = (sem, count[sem], clock)
        for k in rd:
            read.setdefault(k, []).append(e)
        for k in wr:
            wrote[k] = e
            read[k] = []

    def op(q, fn, rd, wr):
        deps(q, rd, wr)
        fn().then_inc(T.sem[own[q]], 1)
        done(q, own[q], 1, rd, wr)

    def dma(q, sem, pairs, rd, wr):
        deps(q, rd, wr)
        for o, i in pairs:
            eng[q].dma_start(o, i).then_inc(T.sem[sem], 16)
        done(q, sem, 16 * len(pairs), rd, wr)

    def tok(name, c0, c1):
        return ["%s.%d" % (name, c) for c in range(c0 // 2, (c1 + 1) // 2)]

    vec, act, pe = g.vector, g.scalar, g.tensor
    order, calls = sends(T, topo, via, rank)
    for t in range(DEP):
        sem = "arr%d" % t
        count[sem] = 0
        for bb in range(NB):
            q = (rank - OFF[bb]) % N
            hop = via[(q, bb)]
            count[sem] += width(T, topo, via, q, bb) if hop is None else len(topo.engines(hop, core))
        wrote[sem] = (sem, count[sem], {sem: count[sem]})

    def wrap(out, col, lhs, src, c0, c1):
        for i in range(16):
            last = pe.matmul(T[out][:, col:col + c1 - c0], T[lhs][:, 15 - i:143 - i], T[src][:, 16 * c0 + i:16 * c1:16],
                             i == 0, i == 15)
        return last

    def flat(out, col, lhs, src, i0, i1, start, stop):
        for i in range(i0, i1):
            last = pe.matmul(T[out][:, col:col + C], T[lhs][:, 15 - i:143 - i], T[src][:, C * i:C * (i + 1)],
                             start and i == i0, stop and i == i1 - 1)
        return last

    dma("y", "lnd", [(T.nd32[:], T.nd0[:])], [], ["nd32"])
    dma("s", "lway", [(T.tk[:, 0:128], T.way[:])], [], ["way"])
    dma("y", "lhs", [(T.hs[:], T.hist[:])], [], ["hs"])
    dma("s", "lbd", [(T.bd32[:], T.bd[:])], [], ["bd32"])
    for k, (c0, c1) in enumerate(CFG["x"]):
        dma("y", "lx%d" % k, [(T.xs[:, 16 * c0:16 * c1], T.x[:, 16 * c0:16 * c1])], [], tok("xs", c0, c1))
    dma("y", "lkid", [(T.tk[:, 128:256], T.kid0[:]), (T.tk[:, 256:384], T.kid1[:])], [], ["kid"])
    for k in range(2):
        dma("y", "lnb%d" % k, [(T.nb32[:, k * S // 2:(k + 1) * S // 2], T.nb[:, k * S // 2:(k + 1) * S // 2])], [],
            tok("nb32", k * C // 2, (k + 1) * C // 2))

    op("g", lambda: g.iota(T.zz[:], [[-16, 8], [0, 16]], 0, 1, allow_small_or_imprecise_dtypes=True), [], ["zz"])
    op("g", lambda: g.iota(T.ki[:], [[0, 1]], 0, 1), [], ["ki"])
    op("g", lambda: g.iota(T.km[:], [[-1, 128]], 0, 1, allow_small_or_imprecise_dtypes=True), [], ["km"])
    op("g", lambda: g.iota(T.kt[:], [[0, V]], 0, 0, allow_small_or_imprecise_dtypes=True), [], ["kt"])
    op("v", lambda: vec.memset(T.fw[:], 0.0), [], ["fw"])
    op("v", lambda: vec.memset(T.d0[:], 0.0), [], ["d0z"])
    for j in range(16):
        op("v", lambda: vec.tensor_scalar(T.rep[:, 128 * j:128 * (j + 1)], T.zz[:], float(j), None, ALU.is_equal),
           ["zz"], ["rep%d" % j])
        if j == 7:
            op("v", lambda: vec.tensor_scalar(T.ei[:], T.ki[:], 15, None, ALU.bitwise_and), ["ki"], ["ei"])
    op("v", lambda: vec.tensor_scalar(T.nec[:], T.ei[:], -1.0, None, ALU.mult), ["ei"], ["nec"])
    op("v", lambda: vec.tensor_copy(T.wb[:], T.tk[:, 0:128]), ["way"], ["wb"])
    tb = ["q0", "q1", "q2", "q3"]
    for k in range(4):
        def rep4():
            for j in range(4 * k, 4 * k + 4):
                last = pe.matmul(T[tb[k]][:, 128 * (j % 4):128 * (j % 4 + 1)], T.rep[:, 128 * j:128 * (j + 1)], T.wb[:],
                                 True, True)
            return last
        op("t", rep4, ["wb"] + ["rep%d" % j for j in range(4 * k, 4 * k + 4)], [tb[k]])

    def apart(k):
        op("s", lambda: act.activation(T.tmp[:, 512 * k:512 * (k + 1)], T[tb[k]][:], ACT.Abs, bias=T.nec[:]),
           ["nec"], [tb[k], "tmp%d" % k])

    for k in range(3):
        apart(k)
    op("v", lambda: vec.tensor_copy(T.ec[:], T.ei[:]), ["ei"], ["ec"])
    op("v", lambda: vec.tensor_scalar(T.idp[:], T.km[:], 0.0, None, ALU.is_equal), ["km"], ["idp"])
    op("v", lambda: vec.tensor_scalar(T.idn[:], T.km[:], 0.0, -1.0, ALU.is_equal, ALU.mult), ["km"], ["idn"])
    op("v", lambda: vec.tensor_copy(T.no0[:], T.nd32[:]), ["nd32"], tok("no0", 0, C))
    op("v", lambda: vec.tensor_scalar(T.fw[:, 15:143:16], T.zz[:, 0:128:16], T.ec[:], None, ALU.is_equal),
       ["zz", "ec"], ["fw"])
    op("v", lambda: vec.tensor_scalar(T.sg[:], T.ec[:], 1.5, 0.5, ALU.is_ge, ALU.subtract), ["ec"], ["sg"])
    op("v", lambda: vec.tensor_scalar(T.lo[:], T.ec[:], 1.5, None, ALU.is_lt), ["ec"], ["lo"])
    for k, bb in enumerate(order):
        op("v", lambda: vec.tensor_copy(T.bdo[:, 16 * k:16 * (k + 1)], T.bd32[:, 16 * bb:16 * (bb + 1)]), ["bd32"], ["bdo%d" % k])
    op("v", lambda: vec.tensor_copy(T.fh[:], T.fw[:]), ["fw"], ["fh"])
    op("v", lambda: vec.tensor_scalar(T.fd[:], T.fw[:], T.sg[:], 2.0, ALU.mult, ALU.mult), ["fw", "sg"], ["fd"])
    op("v", lambda: vec.tensor_scalar(T.f0[:], T.fw[:], T.lo[:], None, ALU.mult), ["fw", "lo"], ["f0"])
    op("v", lambda: vec.tensor_scalar(T.tab[:, 0:1024], T.tmp[:, 0:1024], 0.0, None, ALU.is_equal), ["tmp0", "tmp1"], ["tabv"])

    held, begun = {}, []

    def border(r):
        for pos in range(NB):
            cuts = [(0, 8, "v"), (8, 16, "s")] if len(calls) == 3 and pos >= 2 else [(0, 16, "vs"[pos % 2])]
            for a, b, who in cuts:
                out = T["snd" + r][:, pos * G + 16 * a:pos * G + 16 * b]
                src = T["dw" + r][:, 0:S].indirect(T.bdo[:, 16 * pos + a:16 * pos + b])
                rd, wr = tok("dw" + r, 0, C) + ["bdo%d" % pos], tok("snd" + r, 16 * pos + a, 16 * pos + b)
                if who == "v":
                    op("v", lambda: vec.tensor_copy(out, src), rd, wr)
                else:
                    op("s", lambda: act.activation(out, src, ACT.Copy), rd, wr)
        for call in calls:
            trs, rd = [], []
            for (bb, d, e) in call:
                rid, pid = topo.addr(d, core)
                pos = order.index(bb)
                rd += tok("snd" + r, 16 * pos, 16 * pos + 16)
                if via[(rank, bb)] is None:
                    dst, sem = T["dw" + r][:, S + bb * G:S + (bb + 1) * G], "arr" + r
                else:
                    dst, sem = T["snd" + r][:, bb * G:(bb + 1) * G], "hop%s_%d" % (r, bb)
                trs.append(RemoteDMATransfer(dst_ids=[DstId(rid=rid, pnc=pid)], dma_engine_mask=bits(e), remote_sem=T.sem[sem],
                                             src=T["snd" + r][:, pos * G:(pos + 1) * G], dst=dst))
                count["sent"] = count.get("sent", 0) + len(e)
            deps("g", rd, [])
            g.remote_dma_fused(trs, local_sem=T.sem.sent)

    def stem(word):
        return word.split("@")[0].rstrip("0123456789-")

    def emit(word, t):
        name = stem(word)
        r = str(t)
        if name == "Z":
            apart(int(word[1:]))
            return
        if name == "G":
            border(r)
            return
        if name == "K":
            op("v", lambda: vec.tensor_copy(T.pc[:, 0:256], T.tk[:, 128:384]), ["kid"], ["pch"])
            op("v", lambda: vec.tensor_scalar(T.tab[:, 1024:1536], T.tmp[:, 1024:1536], 0.0, None, ALU.is_equal), ["tmp2"], ["tabw"])
            op("v", lambda: vec.tensor_tensor(T.pc[:, 256:512], T.tk[:, 128:384], T.pc[:, 0:256], ALU.subtract),
               ["kid", "pch"], ["pcl"])
            dma("y", "lkt", [(T.kt[i:128:16, :], T.pc[:, 128 * k:128 * (k + 1)]) for i, k in enumerate((0, 2, 1, 3))],
                ["pch", "pcl"], ["kt"])
            return
        span = word[len(name):].split("@")
        c0, c1 = [int(v) for v in span[0].split("-")]
        last = t == DEP - 1
        n = 16 * (c1 - c0)
        e0, e1 = 16 * c0, 16 * c1
        no, po, dw = T["no" + r], T["po" + r], T["dw" + r]
        window = ["arr" + r] + tok("dw" + r, 0, C)
        qn, gn = "q" + span[-1], "g" + span[-1]
        if name == "L":
            op("v", lambda: vec.tensor_scalar(T.nb16[:, e0:e1], T.nb32[:, e0:e1], float(MID), None, ALU.subtract),
               tok("nb32", c0, c1), tok("nb16", c0, c1))
        if name == "A":
            op("v", lambda: vec.tensor_tensor(dw[:, e0:e1], T.hs[:].indirect(no[:, c0:c1]), T.xs[:, e0:e1], ALU.subtract),
               ["hs"] + tok("xs", c0, c1) + tok("no" + r, c0, c1), tok("dw" + r, c0, c1))
        if name == "Px":
            op("t", lambda: pe.matmul(T[qn][:, 0:n], T.idn[:], T.xs[:, e0:e1], True, False), ["idn"] + tok("xs", c0, c1), [qn])
        if name == "As":
            op("s", lambda: act.activation(T[gn][:, 0:n], T.hs[:].indirect(no[:, c0:c1]), ACT.Copy),
               ["hs"] + tok("no" + r, c0, c1), [gn])
        if name in ("Pa", "Pc"):
            op("t", lambda: pe.matmul(T[qn][:, 0:n], T.idp[:], T[gn][:, 0:n], False, True), ["idp", gn], [qn])
        if name == "Ea":
            op("s", lambda: act.activation(dw[:, e0:e1], T[qn][:, 0:n], ACT.Copy), [], [qn] + tok("dw" + r, c0, c1))
        if name == "Y":
            op("v", lambda: vec.tensor_copy(T.dn[:, e0:e1], dw[:, e0:e1]), tok("dw" + r, c0, c1), tok("dn", c0, c1))
        if name == "B":
            op("v", lambda: vec.tensor_tensor(T.bo[:, e0:e1], T.tab[:].indirect(no[:, c0:c1]), T.nb16[:, e0:e1], ALU.mult),
               ["tabv", "tabw", "tabs"] + tok("nb16", c0, c1) + tok("no" + r, c0, c1), tok("bo", c0, c1))
        if name == "Wp":
            op("t", lambda: wrap("qp", c0, "fh", "bo", c0, c1), ["fh"] + tok("bo", c0, c1), ["qp"])
        if name == "Po":
            op("v", lambda: vec.tensor_scalar(po[:, c0:c1], T.qp[:, c0:c1], float(MID), None, ALU.add), [],
               ["qp"] + tok("po" + r, c0, c1))
        if name == "D":
            op("s", lambda: act.activation(T.ko[:, e0:e1], T.kt[:].indirect(no[:, c0:c1]), ACT.Copy),
               ["kt"] + tok("no" + r, c0, c1), tok("ko", c0, c1))
        if name == "Wk":
            for col, lhs in ((c0, "fd"), (C + c0, "f0")):
                if last:
                    op("t", lambda: flat("qk", col - c0, lhs, "ko", 0, 16, True, True), [lhs] + tok("ko", 0, C), ["qk"])
                else:
                    op("t", lambda: wrap("qk", col, lhs, "ko", c0, c1), [lhs] + tok("ko", c0, c1), ["qk"])
        if name == "Ek":
            op("s", lambda: act.activation(T.d0[:, 2 * c0 + 1:2 * c1:2], T.qk[:, c0:c1], ACT.Copy), ["d0z"],
               ["qk"] + tok("d0", c0, c1))
            op("s", lambda: act.activation(T.d1[:, 2 * c0 + 1:2 * c1:2], T.qk[:, C + c0:C + c1], ACT.Copy), [],
               ["qk"] + tok("d1m", c0, c1))
        if name == "C":
            op("v", lambda: vec.tensor_tensor(T.cmp[:, e0:e1], dw[:].indirect(po[:, c0:c1]), T.dn[:, e0:e1], ALU.is_gt),
               window + tok("dn", c0, c1) + tok("po" + r, c0, c1), tok("cmp", c0, c1))
        if name == "Pd":
            op("t", lambda: pe.matmul(T[qn][:, 0:n], T.idn[:], dw[:, e0:e1], True, False), ["idn"] + tok("dw" + r, c0, c1), [qn])
        if name == "Cs":
            op("s", lambda: act.activation(T[gn][:, 0:n], dw[:].indirect(po[:, c0:c1]), ACT.Copy),
               window + tok("po" + r, c0, c1), [gn])
        if name == "Sc":
            op("s", lambda: act.activation(T.cmp[:, e0:e1], T[qn][:, 0:n], ACT.Sigmoid, bias=-100.0, scale=200.0), [],
               [qn] + tok("cmp", c0, c1))
        if name == "W":
            for c in range(c0, c1):
                held[c] = (qn, c0)
            op("t", lambda: wrap(qn, 0, "fw", "cmp", c0, c1), ["fw"] + tok("cmp", c0, c1), [qn])
        if name in ("Tv", "Ts"):
            bank, base = held[c0]
            out, src = T.d1[:, 2 * c0:2 * c1:2], T[bank][:, c0 - base:c1 - base]
            if name == "Tv":
                op("v", lambda: vec.tensor_scalar(out, src, Q - 0.5, None, ALU.is_ge), [], [bank] + tok("d1s", c0, c1))
            else:
                op("s", lambda: act.activation(out, src, ACT.Sigmoid, bias=-200.0 * (Q - 0.5), scale=200.0), [],
                   [bank] + tok("d1s", c0, c1))
        if name == "N":
            op("v", lambda: vec.tensor_tensor_scan(T.sc[:, 2 * c0:2 * c1], T.d0[:, 2 * c0:2 * c1], T.d1[:, 2 * c0:2 * c1],
                                                   0.0, ALU.mult, ALU.add),
               tok("d0", c0, c1) + tok("d1m", c0, c1) + tok("d1s", c0, c1), tok("sc", c0, c1))
        if name == "M":
            op("v", lambda: vec.tensor_scalar(no[:, c0:c1], T.sc[:, 2 * c0 + 1:2 * c1:2], 0.25, None, ALU.add),
               tok("sc", c0, c1), tok("no" + r, c0, c1))
        if name == "F":
            begun.append(c1 - c0)
            op("t", lambda: flat("q0", 0, "fw", "cmp", c0 // 6, c1 // 6, len(begun) == 1, sum(begun) == C),
               ["fw"] + tok("cmp", c0, c1), ["q0"])

    for w in CFG["open"].split():
        emit(w, 0)
    op("s", lambda: act.activation(T.tab[:, 1536:V], T.tmp[:, 1536:V], ACT.Sigmoid, bias=100.0, scale=-200.0), ["tmp3"], ["tabs"])
    for w in CFG["wait0"].split():
        emit(w, 0)
    for t in range(DEP - 1):
        for w in CFG["step"].split():
            emit(w, t if stem(w) in ("C", "Cs", "Ek", "Pc", "Sc", "W", "Tv", "Ts", "N") else t + 1)
        for w in CFG["wait3" if t == DEP - 2 else "wait"].split():
            emit(w, t + 1)
    for w in CFG["last"].split():
        emit(w, DEP - 1)
    op("v", lambda: vec.tensor_scalar(T.yt[:], T.q0[:, 0:C], Q - 0.5, None, ALU.is_ge), [], ["q0", "yt"])
    op("v", lambda: vec.tensor_tensor(T.yu[:], T.yt[:], T.qk[:, 0:C], ALU.mult), ["yt"], ["qk", "yu"])
    op("v", lambda: vec.tensor_tensor(T.yv[:], T.yu[:], T.qk[:, C:2 * C], ALU.add), ["yu"], ["qk", "yv"])
    dma("y", "ly", [(T.y[:], T.yv[:])], ["yv"], ["y"])
    for sem in sorted(count, key=lambda s: s == "ly"):
        if waited.get(sem, 0) < count[sem]:
            g.wait_ge(T.sem[sem], count[sem])
